import numpy as np
import ml_dtypes


def mxq(x, axis, fmt="e4m3"):
    dtype, down = {"e4m3": (ml_dtypes.float8_e4m3fn, 7), "e5m2": (ml_dtypes.float8_e5m2, 14)}[fmt]
    v = np.moveaxis(np.asarray(x, np.float32).astype(ml_dtypes.bfloat16).astype(np.float64), axis, -1)
    blocks = v.reshape(v.shape[:-1] + (-1, 32))
    amax = np.abs(blocks).max(-1, keepdims=True)
    byte = np.maximum(np.where(amax > 0, np.frexp(amax)[1] - 1 + 127, 0) - down, 1)
    scale = np.exp2(byte - 127.0)
    codes = (blocks / scale).astype(np.float32).astype(dtype).astype(np.float64)
    return np.moveaxis((codes * scale).reshape(v.shape), -1, axis)


WIDE = False


def mx_kscale(k):
    if not WIDE:
        return np.ones(k)
    levels = np.array([10, -10, 5, -5, 0])
    if k % 512:
        return np.exp2(np.random.permutation(np.resize(levels, k // 32))).repeat(32)
    a = np.empty((k // 512, 16))
    for p in range(k // 512):
        a[p, :8] = np.random.permutation(np.resize(levels, 8))
        for g in range(8):
            far = levels[np.abs(levels - a[p, g]) >= 10]
            a[p, g + 8] = far[np.random.randint(len(far))]
    return np.exp2(a.ravel()).repeat(32)


BF16 = ml_dtypes.bfloat16


def bf(x):
    return np.asarray(x, np.float32).astype(BF16)


def f64(x):
    return np.asarray(x).astype(np.float64)


E2M1 = np.array([0.0, 0.5, 1.0, 1.5, 2.0, 3.0, 4.0, 6.0, -0.0, -0.5, -1.0, -1.5, -2.0, -3.0, -4.0, -6.0])


def pack_weight(w, fmt):
    k, n = w.shape
    w = f64(bf(w)).reshape(k // 32, 32, n)
    amax = np.abs(w).max(1)
    if fmt == "e4m3":
        byte = np.frexp(amax)[1] - 1 + 127 - 7
    else:
        mant, ex = np.frexp(amax / 6.0)
        byte = np.where(mant > 0.5, ex, ex - 1) + 127
    byte = np.clip(np.where(amax > 0, byte, 1), 1, 254)
    scaled = (w * np.exp2(127.0 - byte)[:, None, :]).reshape(k, n).astype(np.float32)
    by_word = np.ascontiguousarray(scaled.reshape(k // 512, 128, 4, n).transpose(0, 1, 3, 2))
    if fmt == "e4m3":
        words = by_word.astype(ml_dtypes.float8_e4m3fn).view(np.uint8)
    else:
        c = by_word.astype(ml_dtypes.float4_e2m1fn).view(np.uint8) & 0xF
        words = c[..., 0::2] | (c[..., 1::2] << 4)
    return np.ascontiguousarray(words), np.ascontiguousarray(byte.astype(np.uint8).reshape(k // 512, 16, n))


def unpack_weight(words, scales, fmt):
    g, p, n, _ = words.shape
    if fmt == "e4m3":
        vals = np.ascontiguousarray(words).view(ml_dtypes.float8_e4m3fn).astype(np.float64)
    else:
        nib = np.empty((g, p, n, 4), np.uint8)
        nib[..., 0::2] = words & 0xF
        nib[..., 1::2] = words >> 4
        vals = E2M1[nib]
    vals = vals * np.repeat(np.exp2(scales.astype(np.float64) - 127.0), 8, axis=1)[..., None]
    return vals.transpose(0, 1, 3, 2).reshape(g * 512, n)
def pack4(w):
    words, scales = pack_weight(w, "e2m1")
    return words.reshape(words.shape[0], 128, -1), scales


def unpack4(words, scales):
    return unpack_weight(words.reshape(words.shape[0], 128, -1, 2), scales, "e2m1")


def planes(Y):
    n, m = Y.shape
    b = f64(bf(Y)).reshape(n // 32, 32, m)
    amax = np.abs(b).max(1)
    byte = np.clip(np.where(amax > 0, np.frexp(amax)[1] - 1 + 127 - 7, 1), 1, 254)
    codes = (b * np.exp2(127.0 - byte)[:, None, :]).reshape(n, m).astype(np.float32).astype(ml_dtypes.float8_e4m3fn).view(np.uint8)
    words = codes.reshape(n // 512, 128, 4, m).transpose(0, 1, 3, 2)
    return np.ascontiguousarray(words), np.ascontiguousarray(byte.astype(np.uint8).reshape(n // 512, 16, m))


T, S, C, P = 1536, 2048, 512, 1024


def setup_inputs():
    s = mx_kscale(S)
    t = mx_kscale(C)
    env = np.exp(0.8 * np.random.randn(T, 1))
    currents = env * np.random.randn(T, S) * s[None, :]
    eeg = env * np.random.randn(T, C) * t[None, :]
    lead = np.random.randn(S, C) / np.sqrt(S) / s[:, None] * t[None, :]
    inv = np.random.randn(C, S) / np.sqrt(C) / t[:, None]
    lead_words, lead_scales = pack4(lead)
    inv_words, inv_scales = pack4(inv)
    weight = np.exp(0.3 * np.random.randn(S))
    return {"currents": bf(currents), "eeg": bf(eeg),
            "lead_words": lead_words, "lead_scales": lead_scales,
            "inv_words": inv_words, "inv_scales": inv_scales,
            "weight": bf(weight)}

def reference(currents, eeg, lead_words, lead_scales, inv_words, inv_scales, weight):
    L = unpack4(lead_words, lead_scales)
    G = unpack4(inv_words, inv_scales)
    R = f64(eeg) - (mxq(f64(currents), 1, "e4m3") @ L)
    Z = (mxq(R, 1, "e4m3") @ G) * f64(weight)
    y = 0.5 * (Z[:, :P] + Z[:, P:])
    Y = y.reshape(T, P)
    words, scales = planes(Y)
    return y, words, scales

@@ -1,0 +1,400 @@
+from contextlib import ExitStack
+
+import concourse.mybir as mybir
+from concourse.masks import make_identity
+
+T, S, C, NP = 1536, 2048, 512, 1024
+FLOPS = 2 * T * S * C + 2 * T * C * S
+
+F32 = mybir.dt.float32
+BF16 = mybir.dt.bfloat16
+U32 = mybir.dt.uint32
+I32 = mybir.dt.int32
+U8 = mybir.dt.uint8
+FP8X4 = mybir.dt.float8_e4m3fn_x4
+FP4X4 = mybir.dt.float4_e2m1fn_x4
+ALU = mybir.AluOpType
+COPY = mybir.ActivationFunctionType.Copy
+
+P = 128
+GROUPS = T // 512
+TILES = T // P
+HALF = 512
+
+
+def tile_eeg_residual_parcel_averages_h1_kernel(
+    tc, currents, eeg, lead_words, lead_scales, inv_words, inv_scales, weight, out_0, out_1, out_2
+):
+    nc = tc.nc
+    with ExitStack() as ctx:
+        keep = ctx.enter_context(tc.tile_pool(name="keep", bufs=1))
+        work = ctx.enter_context(tc.tile_pool(name="work", bufs=3))
+        psum = ctx.enter_context(tc.psum_pool(name="psum", bufs=1))
+        ctx.enter_context(tc.manual_schedule())
+
+        banks_taken = []
+
+        def next_bank():
+            name = "bank%d" % (len(banks_taken) % 8)
+            banks_taken.append(name)
+            return psum.tile([P, 512], F32, name=name)
+
+        def kept(shape, dtype, name):
+            return keep.tile(shape, dtype, name=name, align_bytes=64)
+
+        def rotating(shape, dtype, name):
+            return work.tile(shape, dtype, name=name, align_bytes=64)
+
+        def by_slot(dram, g):
+            return dram[512 * g : 512 * (g + 1), :].rearrange("(p t) c -> p t c", t=4)
+
+        w_rows = kept([P, P], BF16, "w_rows")
+        nc.gpsimd.memset(w_rows[:], 0.0)
+        nc.gpsimd.dma_start(out=w_rows[0:16, :], in_=weight.rearrange("(j p) -> j p", p=P))
+        ident = kept([P, P], F32, "ident")
+        make_identity(nc, ident[:])
+
+        lead_plane = kept([P, 4 * C], U8, "lead_plane")
+        inv_plane = kept([P, S], U8, "inv_plane")
+        nc.vector.memset(lead_plane[:].bitcast(I32), 0)
+        nc.vector.memset(inv_plane[:].bitcast(I32), 0)
+
+        lead_codes = kept([P, 4 * 2 * C], U8, "lead_codes")
+        inv_codes = kept([P, 2 * S], U8, "inv_codes")
+        x = [kept([P, S], BF16, "x%d" % i) for i in range(TILES)]
+        e = [kept([P, 2, C], BF16, "e%d" % g) for g in range(TILES // 2)]
+
+        def load_x(i, cols):
+            nc.sync.dma_start(out=x[i][:, cols], in_=by_slot(currents, i // 4)[:, i % 4, cols])
+
+        def load_e(k):
+            nc.sync.dma_start(out=e[k][:], in_=by_slot(eeg, k // 2)[:, 2 * (k % 2) : 2 * (k % 2) + 2, :])
+
+        load_x(0, slice(0, S // 2))
+        load_x(0, slice(S // 2, S))
+        for q in range(4):
+            nc.sync.dma_start(
+                out=lead_plane[32 * q : 32 * q + 4, :].bitcast(I32).rearrange("r (g n) -> r g n", g=4),
+                in_=lead_scales.bitcast(I32)[:, 4 * q : 4 * q + 4, :].rearrange("g r n -> r g n"),
+            )
+        load_x(1, slice(0, S))
+        nc.sync.dma_start(
+            out=lead_codes[:].bitcast(I32).rearrange("p (g n) -> p g n", g=4),
+            in_=lead_words.bitcast(I32).rearrange("g p n -> p g n"),
+        )
+        load_e(0)
+        load_x(2, slice(0, S))
+        for q in range(4):
+            nc.sync.dma_start(
+                out=inv_plane[32 * q : 32 * q + 4, :].bitcast(I32),
+                in_=inv_scales.bitcast(I32)[0, 4 * q : 4 * q + 4, :],
+            )
+        nc.sync.dma_start(out=inv_codes[:].bitcast(I32), in_=inv_words.bitcast(I32)[0])
+        for i in range(3, TILES):
+            load_x(i, slice(0, S))
+            if i % 2 == 1 and i < TILES - 1:
+                load_e(i // 2)
+        load_e(TILES // 2 - 1)
+
+        w_half = kept([P, P], F32, "w_half")
+        w_col = kept([P, 16], F32, "w_col")
+        w_wide = [kept([P, HALF], F32, "w_wide%d" % h) for h in range(2)]
+        nc.scalar.activation(out=w_half[:], in_=w_rows[:], func=COPY, scale=0.5)
+
+        def weight_columns():
+            bank = next_bank()
+            nc.tensor.transpose(bank[:, 0:P], w_half[:], ident[:])
+            nc.vector.tensor_copy(out=w_col[:], in_=bank[:, 0:16])
+
+        def weight_rows():
+            for h in range(2):
+                bank = next_bank()
+                for j in range(4):
+                    col = w_col[:, 8 * h + j : 8 * h + j + 1].to_broadcast([P, P])
+                    nc.tensor.transpose(bank[:, P * j : P * (j + 1)], col, ident[:])
+                nc.scalar.copy(out=w_wide[h][:], in_=bank[:])
+
+        r_codes = [kept([P, 512], U32, "r_codes%d" % g) for g in range(GROUPS)]
+        r_plane = [kept([P, 512], U8, "r_plane%d" % g) for g in range(GROUPS)]
+        y_low = [kept([P, 4, HALF], F32, "y_low%d" % g) for g in range(GROUPS)]
+        y_high = [[kept([P, 4, 256], F32, "y_high%d_%d" % (g, h)) for h in range(2)] for g in range(GROUPS)]
+        y_bf = [[kept([P, HALF, 4], BF16, "y_bf%d_%d" % (g, h)) for h in range(2)] for g in range(GROUPS)]
+        y_codes = [kept([P, NP], U32, "y_codes%d" % g) for g in range(GROUPS)]
+        y_plane = [kept([P, NP], U8, "y_plane%d" % g) for g in range(GROUPS)]
+
+        st = {}
+
+        def put(key, val):
+            st.setdefault(key, val)
+
+        def turn_x(i, h):
+            words = x[i][:].bitcast(F32)
+            bank = next_bank()
+            for gl in range(2):
+                g = 2 * h + gl
+                for u in range(2):
+                    slot = 2 * gl + u
+                    nc.tensor.transpose(
+                        bank[:, P * slot : P * (slot + 1)], words[:, 256 * g + u : 256 * (g + 1) : 2], ident[:]
+                    )
+            put(("xt", i, h), bank)
+
+        def copy_x(i, h):
+            if h == 0:
+                put(("xg", i), rotating([P, S], BF16, "x_grouped"))
+            grouped = st[("xg", i)]
+            nc.scalar.copy(
+                out=grouped[:, 1024 * h : 1024 * (h + 1)].bitcast(F32).rearrange("p (g r u) -> p g r u", g=2, u=2),
+                in_=st[("xt", i, h)][:].rearrange("p (g u r) -> p g r u", g=2, u=2),
+            )
+
+        def quantize_x(i):
+            codes = rotating([P, 512], U32, "x_codes")
+            plane = rotating([P, 512], U8, "x_plane")
+            nc.vector.quantize_mx(out=codes[:].bitcast(FP8X4), scales=plane[:], in_=st[("xg", i)][:])
+            put(("xq", i), (codes, plane))
+
+        def predict(i):
+            codes, plane = st[("xq", i)]
+            bank = next_bank()
+            for g in range(4):
+                cols = slice(P * g, P * (g + 1))
+                nc.tensor.matmul_mx(
+                    out=bank[:],
+                    lhsT=codes[:, cols].bitcast(FP8X4),
+                    lhsT_scale=plane[:, cols],
+                    rhs=lead_codes[:, 2 * C * g : 2 * C * (g + 1)].bitcast(FP4X4),
+                    rhs_scale=lead_plane[:, C * g : C * (g + 1)],
+                    start=(g == 0),
+                    stop=(g == 3),
+                )
+            put(("pred", i), bank)
+
+        def residual(i):
+            r = rotating([P, C], BF16, "r")
+            nc.vector.tensor_tensor(
+                out=r[:].rearrange("p (u q e) -> p u q e", u=2, e=2),
+                in0=e[i // 2][:, i % 2, :].rearrange("p (q u e) -> p u q e", u=2, e=2),
+                in1=st[("pred", i)][:].rearrange("p (q u e) -> p u q e", u=2, e=2),
+                op=ALU.subtract,
+            )
+            put(("r", i), r)
+
+        def turn_r(i):
+            words = st[("r", i)][:].bitcast(F32)
+            bank = next_bank()
+            for u in range(2):
+                nc.tensor.transpose(bank[:, P * u : P * (u + 1)], words[:, P * u : P * (u + 1)], ident[:])
+            put(("rt", i), bank)
+
+        def copy_r(i):
+            grouped = rotating([P, C], BF16, "r_grouped")
+            nc.scalar.copy(
+                out=grouped[:].bitcast(F32).rearrange("p (r u) -> p r u", u=2),
+                in_=st[("rt", i)][:, 0 : 2 * P].rearrange("p (u r) -> p r u", u=2),
+            )
+            put(("rg", i), grouped)
+
+        def quantize_r(i):
+            g, cols = i // 4, slice(P * (i % 4), P * (i % 4 + 1))
+            nc.vector.quantize_mx(
+                out=r_codes[g][:, cols].bitcast(FP8X4), scales=r_plane[g][:, cols], in_=st[("rg", i)][:]
+            )
+
+        def low_matmul(i):
+            g, cols = i // 4, slice(P * (i % 4), P * (i % 4 + 1))
+            pair = []
+            for h in range(2):
+                bank = next_bank()
+                n0 = NP * h
+                nc.tensor.matmul_mx(
+                    out=bank[:],
+                    lhsT=r_codes[g][:, cols].bitcast(FP8X4),
+                    lhsT_scale=r_plane[g][:, cols],
+                    rhs=inv_codes[:, 2 * n0 : 2 * (n0 + HALF)].bitcast(FP4X4),
+                    rhs_scale=inv_plane[:, n0 : n0 + HALF],
+                    start=True,
+                    stop=True,
+                )
+                pair.append(bank)
+            put(("low", i), pair)
+
+        def low_weigh(i):
+            pair = []
+            for h in range(2):
+                z = rotating([P, HALF], F32, "z_low%d" % h)
+                nc.vector.tensor_tensor(out=z[:], in0=st[("low", i)][h][:], in1=w_wide[h][:], op=ALU.mult)
+                pair.append(z)
+            put(("lowz", i), pair)
+
+        def low_add(i):
+            g, t = i // 4, i % 4
+            a, b = st[("lowz", i)]
+            nc.vector.tensor_tensor(out=y_low[g][:, t, :], in0=a[:], in1=b[:], op=ALU.add)
+            nc.sync.dma_start(out=by_slot(out_0, g)[:, t, 0:HALF], in_=y_low[g][:, t, :])
+
+        def cast_from_sbuf(on_vector, dst, src):
+            out = dst.rearrange("p (c i) t -> p c t i", i=4)
+            in_ = src.rearrange("p t (c i) -> p c t i", i=4)
+            if on_vector:
+                nc.vector.tensor_copy(out=out, in_=in_)
+            else:
+                nc.scalar.copy(out=out, in_=in_)
+
+        def low_cast(g, j, on_vector=False):
+            cols = slice(P * j, P * (j + 1))
+            cast_from_sbuf(on_vector, y_bf[g][0][:, cols, :], y_low[g][:, :, cols])
+
+        def high_matmul(n):
+            g, j = n // 4, 4 + n % 4
+            pair = []
+            for h in range(2):
+                bank = next_bank()
+                n0 = NP * h + P * j
+                nc.tensor.matmul_mx(
+                    out=bank[:],
+                    lhsT=inv_codes[:, 2 * n0 : 2 * (n0 + P)].bitcast(FP4X4),
+                    lhsT_scale=inv_plane[:, n0 : n0 + P],
+                    rhs=r_codes[g][:].bitcast(FP8X4),
+                    rhs_scale=r_plane[g][:],
+                    start=True,
+                    stop=True,
+                )
+                pair.append(bank)
+            put(("high", n), pair)
+
+        def high_left(n):
+            j = 4 + n % 4
+            z = rotating([P, 512], F32, "z_high")
+            nc.scalar.activation(out=z[:], in_=st[("high", n)][0][:], func=COPY, scale=w_col[:, j : j + 1])
+            put(("highz", n), z)
+
+        def high_sum(n):
+            j = 12 + n % 4
+            yt = rotating([P, 512], F32, "y_turned")
+            nc.vector.scalar_tensor_tensor(
+                out=yt[:],
+                in0=st[("high", n)][1][:],
+                scalar=w_col[:, j : j + 1],
+                in1=st[("highz", n)][:],
+                op0=ALU.mult,
+                op1=ALU.add,
+            )
+            put(("yt", n), yt)
+
+        def turn_y(n):
+            bank = next_bank()
+            for t in range(4):
+                cols = slice(P * t, P * (t + 1))
+                nc.tensor.transpose(bank[:, cols], st[("yt", n)][:, cols], ident[:])
+            put(("y", n), bank)
+
+        def copy_y(n, cast=True):
+            g, j = n // 4, n % 4
+            dst = y_high[g][j // 2]
+            cols = slice(P * (j % 2), P * (j % 2 + 1))
+            bank = st[("y", n)][:].rearrange("p (t m) -> p t m", t=4)
+            nc.scalar.copy(out=dst[:, :, cols], in_=bank)
+            if cast:
+                nc.scalar.copy(out=y_bf[g][1][:, P * j : P * (j + 1), :], in_=bank.rearrange("p t m -> p m t"))
+            if j % 2 == 1:
+                c0 = HALF + 256 * (j // 2)
+                nc.sync.dma_start(out=by_slot(out_0, g)[:, :, c0 : c0 + 256], in_=dst[:])
+
+        def high_cast(n):
+            g, j = n // 4, n % 4
+            src = y_high[g][j // 2][:, :, P * (j % 2) : P * (j % 2 + 1)]
+            cast_from_sbuf(True, y_bf[g][1][:, P * j : P * (j + 1), :], src)
+
+        def quantize_y(g, h):
+            cols = slice(HALF * h, HALF * (h + 1))
+            nc.vector.quantize_mx(
+                out=y_codes[g][:, cols].bitcast(FP8X4),
+                scales=y_plane[g][:, cols],
+                in_=y_bf[g][h][:].rearrange("p m t -> p (m t)"),
+            )
+            nc.sync.dma_start(
+                out=out_1[g].rearrange("p m t -> p (m t)").bitcast(I32)[:, cols],
+                in_=y_codes[g][:, cols].bitcast(I32),
+            )
+
+        def store_plane(g):
+            for q in range(4):
+                nc.sync.dma_start(
+                    out=out_2.bitcast(I32)[g, 4 * q : 4 * q + 4, :],
+                    in_=y_plane[g][32 * q : 32 * q + 4, :].bitcast(I32),
+                )
+
+        def live(i):
+            return 0 <= i < TILES
+
+        def when(fn, i, *more):
+            if 0 <= i < TILES:
+                fn(i, *more)
+
+        def finish_low(g):
+            quantize_y(g, 0)
+
+        def finish_high(g):
+            quantize_y(g, 1)
+            store_plane(g)
+
+        for s in range(TILES + 2):
+            n = s - 5
+            when(turn_x, s, 0)
+            when(turn_r, s - 2)
+            when(turn_x, s, 1)
+            if s == 0:
+                weight_columns()
+            when(turn_y, n - 2)
+            when(copy_x, s, 0)
+            when(copy_r, s - 2)
+            when(copy_x, s, 1)
+            when(copy_y, n - 2)
+            if s == 1:
+                weight_rows()
+            when(high_sum, n - 1)
+            when(quantize_r, s - 2)
+            when(low_add, s - 3)
+            when(quantize_x, s)
+            if s - 6 >= 0:
+                low_cast((s - 6) // 4, (s - 6) % 4)
+            if s == 10:
+                finish_low(0)
+            if s == 11:
+                finish_high(0)
+            when(predict, s - 1)
+            when(low_matmul, s - 2)
+            when(high_matmul, n)
+            when(residual, s - 1)
+            when(low_weigh, s - 2)
+            when(high_left, n)
+        high_matmul(9)
+        high_left(9)
+        high_sum(8)
+        low_add(11)
+        high_matmul(10)
+        high_left(10)
+        high_sum(9)
+        turn_y(7)
+        turn_y(8)
+        high_matmul(11)
+        high_left(11)
+        copy_y(7)
+        high_sum(10)
+        finish_low(1)
+        high_sum(11)
+        turn_y(9)
+        turn_y(10)
+        copy_y(8, False)
+        copy_y(9, False)
+        finish_high(1)
+        for j in range(4):
+            low_cast(2, j, True)
+        turn_y(11)
+        copy_y(10)
+        copy_y(11)
+        finish_low(2)
+        high_cast(8)
+        high_cast(9)
+        finish_high(2)

@@ -48,16 +48,16 @@ def tile_eeg_residual_parcel_averages_h1_kernel(
         def by_slot(dram, g):
             return dram[512 * g : 512 * (g + 1), :].rearrange("(p t) c -> p t c", t=4)
 
-        w_rows = kept([P, P], BF16, "w_rows")
-        nc.gpsimd.memset(w_rows[:], 0.0)
-        nc.gpsimd.dma_start(out=w_rows[0:16, :], in_=weight.rearrange("(j p) -> j p", p=P))
+        w_rows = kept([16, P], BF16, "w_rows")
+        w_half = kept([P, P], F32, "w_half")
         ident = kept([P, P], F32, "ident")
-        make_identity(nc, ident[:])
 
         lead_plane = kept([P, 4 * C], U8, "lead_plane")
         inv_plane = kept([P, S], U8, "inv_plane")
         nc.vector.memset(lead_plane[:].bitcast(I32), 0)
-        nc.vector.memset(inv_plane[:].bitcast(I32), 0)
+        nc.vector.memset(w_half[:], 0.0)
+        make_identity(nc, ident[:])
+        nc.gpsimd.memset(inv_plane[:].bitcast(I32), 0)
 
         lead_codes = kept([P, 4 * 2 * C], U8, "lead_codes")
         inv_codes = kept([P, 2 * S], U8, "inv_codes")
@@ -71,6 +71,7 @@ def tile_eeg_residual_parcel_averages_h1_kernel(
             nc.sync.dma_start(out=e[k][:], in_=by_slot(eeg, k // 2)[:, 2 * (k % 2) : 2 * (k % 2) + 2, :])
 
         load_x(0, slice(0, S // 2))
+        nc.sync.dma_start(out=w_rows[:], in_=weight.rearrange("(j p) -> j p", p=P))
         load_x(0, slice(S // 2, S))
         for q in range(4):
             nc.sync.dma_start(
@@ -96,10 +97,9 @@ def tile_eeg_residual_parcel_averages_h1_kernel(
                 load_e(i // 2)
         load_e(TILES // 2 - 1)
 
-        w_half = kept([P, P], F32, "w_half")
         w_col = kept([P, 16], F32, "w_col")
         w_wide = [kept([P, HALF], F32, "w_wide%d" % h) for h in range(2)]
-        nc.scalar.activation(out=w_half[:], in_=w_rows[:], func=COPY, scale=0.5)
+        nc.scalar.activation(out=w_half[0:16, :], in_=w_rows[:], func=COPY, scale=0.5)
 
         def weight_columns():
             bank = next_bank()
@@ -301,17 +301,17 @@ def tile_eeg_residual_parcel_averages_h1_kernel(
                 c0 = HALF + 256 * (j // 2)
                 nc.sync.dma_start(out=by_slot(out_0, g)[:, :, c0 : c0 + 256], in_=dst[:])
 
-        def high_cast(n):
+        def high_cast(n, on_vector=True):
             g, j = n // 4, n % 4
             src = y_high[g][j // 2][:, :, P * (j % 2) : P * (j % 2 + 1)]
-            cast_from_sbuf(True, y_bf[g][1][:, P * j : P * (j + 1), :], src)
+            cast_from_sbuf(on_vector, y_bf[g][1][:, P * j : P * (j + 1), :], src)
 
-        def quantize_y(g, h):
-            cols = slice(HALF * h, HALF * (h + 1))
+        def quantize_y(g, h, c0=0, c1=HALF):
+            cols = slice(HALF * h + c0, HALF * h + c1)
             nc.vector.quantize_mx(
                 out=y_codes[g][:, cols].bitcast(FP8X4),
                 scales=y_plane[g][:, cols],
-                in_=y_bf[g][h][:].rearrange("p m t -> p (m t)"),
+                in_=y_bf[g][h][:, c0:c1, :].rearrange("p m t -> p (m t)"),
             )
             nc.sync.dma_start(
                 out=out_1[g].rearrange("p m t -> p (m t)").bitcast(I32)[:, cols],
@@ -339,7 +339,7 @@ def tile_eeg_residual_parcel_averages_h1_kernel(
             quantize_y(g, 1)
             store_plane(g)
 
-        for s in range(TILES + 2):
+        for s in range(TILES + 1):
             n = s - 5
             when(turn_x, s, 0)
             when(turn_r, s - 2)
@@ -369,32 +369,49 @@ def tile_eeg_residual_parcel_averages_h1_kernel(
             when(residual, s - 1)
             when(low_weigh, s - 2)
             when(high_left, n)
+        turn_r(11)
+        turn_y(6)
+        copy_r(11)
+        high_sum(7)
+        turn_y(7)
+        quantize_r(11)
+        low_cast(1, 3)
+        copy_y(6)
+        copy_y(7)
+        low_add(10)
+        finish_low(1)
+        low_matmul(11)
+        high_matmul(8)
         high_matmul(9)
+        low_weigh(11)
+        high_left(8)
         high_left(9)
-        high_sum(8)
-        low_add(11)
         high_matmul(10)
         high_left(10)
+        finish_high(1)
+        high_sum(8)
+        low_add(11)
         high_sum(9)
-        turn_y(7)
-        turn_y(8)
         high_matmul(11)
         high_left(11)
-        copy_y(7)
-        high_sum(10)
-        finish_low(1)
-        high_sum(11)
+        for j in range(1):
+            low_cast(2, j)
+        turn_y(8)
         turn_y(9)
-        turn_y(10)
+        high_sum(10)
+        high_sum(11)
         copy_y(8, False)
         copy_y(9, False)
-        finish_high(1)
-        for j in range(4):
-            low_cast(2, j, True)
+        turn_y(10)
         turn_y(11)
-        copy_y(10)
-        copy_y(11)
+        for j in range(1, 4):
+            low_cast(2, j, True)
+        copy_y(10, False)
+        copy_y(11, True)
         finish_low(2)
         high_cast(8)
         high_cast(9)
-        finish_high(2)
+        high_cast(10)
+        quantize_y(2, 1, 0, 256)
+        quantize_y(2, 1, 256, HALF)
+        store_plane(2)

@@ -20,6 +20,7 @@ P = 128
 GROUPS = T // 512
 TILES = T // P
 HALF = 512
+SORTED = range(5, 9)
 
 
 def tile_eeg_residual_parcel_averages_h1_kernel(
@@ -127,6 +128,16 @@ def tile_eeg_residual_parcel_averages_h1_kernel(
         def put(key, val):
             st.setdefault(key, val)
 
+        def sort_x(i):
+            if i not in SORTED:
+                return
+            dealt = rotating([P, S // 2], F32, "x_dealt")
+            nc.scalar.copy(
+                out=dealt[:].rearrange("p (g u q) -> p g u q", g=4, u=2),
+                in_=x[i][:].bitcast(F32).rearrange("p (g q u) -> p g u q", g=4, u=2),
+            )
+            put(("xs", i), dealt)
+
         def turn_x(i, h):
             words = x[i][:].bitcast(F32)
             bank = next_bank()
@@ -134,9 +145,11 @@ def tile_eeg_residual_parcel_averages_h1_kernel(
                 g = 2 * h + gl
                 for u in range(2):
                     slot = 2 * gl + u
-                    nc.tensor.transpose(
-                        bank[:, P * slot : P * (slot + 1)], words[:, 256 * g + u : 256 * (g + 1) : 2], ident[:]
-                    )
+                    if i in SORTED:
+                        src = st[("xs", i)][:, 256 * g + P * u : 256 * g + P * (u + 1)]
+                    else:
+                        src = words[:, 256 * g + u : 256 * (g + 1) : 2]
+                    nc.tensor.transpose(bank[:, P * slot : P * (slot + 1)], src, ident[:])
             put(("xt", i, h), bank)
 
         def copy_x(i, h):
@@ -353,22 +366,23 @@ def tile_eeg_residual_parcel_averages_h1_kernel(
             when(copy_y, n - 2)
             if s == 1:
                 weight_rows()
+            when(sort_x, s + 2)
             when(high_sum, n - 1)
             when(quantize_r, s - 2)
             when(low_add, s - 3)
             when(quantize_x, s)
             if s - 6 >= 0:
                 low_cast((s - 6) // 4, (s - 6) % 4)
-            if s == 10:
-                finish_low(0)
-            if s == 11:
-                finish_high(0)
             when(predict, s - 1)
             when(low_matmul, s - 2)
             when(high_matmul, n)
             when(residual, s - 1)
             when(low_weigh, s - 2)
             when(high_left, n)
+            if s == 9:
+                finish_low(0)
+            if s == 10:
+                finish_high(0)
         turn_r(11)
         turn_y(6)
         copy_r(11)

from contextlib import ExitStack

import concourse.mybir as mybir
from concourse.masks import make_identity

T, S, C, NP = 1536, 2048, 512, 1024
FLOPS = 2 * T * S * C + 2 * T * C * S

F32 = mybir.dt.float32
BF16 = mybir.dt.bfloat16
U32 = mybir.dt.uint32
I32 = mybir.dt.int32
U8 = mybir.dt.uint8
FP8X4 = mybir.dt.float8_e4m3fn_x4
FP4X4 = mybir.dt.float4_e2m1fn_x4
ALU = mybir.AluOpType
COPY = mybir.ActivationFunctionType.Copy

P = 128
GROUPS = T // 512
TILES = T // P
HALF = 512
SORTED = range(5, 9)


def tile_eeg_residual_parcel_averages_h1_kernel(
    tc, currents, eeg, lead_words, lead_scales, inv_words, inv_scales, weight, out_0, out_1, out_2
):
    nc = tc.nc
    with ExitStack() as ctx:
        keep = ctx.enter_context(tc.tile_pool(name="keep", bufs=1))
        work = ctx.enter_context(tc.tile_pool(name="work", bufs=3))
        psum = ctx.enter_context(tc.psum_pool(name="psum", bufs=1))
        ctx.enter_context(tc.manual_schedule())

        banks_taken = []

        def next_bank():
            name = "bank%d" % (len(banks_taken) % 8)
            banks_taken.append(name)
            return psum.tile([P, 512], F32, name=name)

        def kept(shape, dtype, name):
            return keep.tile(shape, dtype, name=name, align_bytes=64)

        def rotating(shape, dtype, name):
            return work.tile(shape, dtype, name=name, align_bytes=64)

        def by_slot(dram, g):
            return dram[512 * g : 512 * (g + 1), :].rearrange("(p t) c -> p t c", t=4)

        w_rows = kept([16, P], BF16, "w_rows")
        w_half = kept([P, P], F32, "w_half")
        ident = kept([P, P], F32, "ident")

        lead_plane = kept([P, 4 * C], U8, "lead_plane")
        inv_plane = kept([P, S], U8, "inv_plane")
        nc.vector.memset(lead_plane[:].bitcast(I32), 0)
        nc.vector.memset(w_half[:], 0.0)
        make_identity(nc, ident[:])
        nc.gpsimd.memset(inv_plane[:].bitcast(I32), 0)

        lead_codes = kept([P, 4 * 2 * C], U8, "lead_codes")
        inv_codes = kept([P, 2 * S], U8, "inv_codes")
        x = [kept([P, S], BF16, "x%d" % i) for i in range(TILES)]
        e = [kept([P, 2, C], BF16, "e%d" % g) for g in range(TILES // 2)]

        def load_x(i, cols):
            nc.sync.dma_start(out=x[i][:, cols], in_=by_slot(currents, i // 4)[:, i % 4, cols])

        def load_e(k):
            nc.sync.dma_start(out=e[k][:], in_=by_slot(eeg, k // 2)[:, 2 * (k % 2) : 2 * (k % 2) + 2, :])

        load_x(0, slice(0, S // 2))
        nc.sync.dma_start(out=w_rows[:], in_=weight.rearrange("(j p) -> j p", p=P))
        load_x(0, slice(S // 2, S))
        for q in range(4):
            nc.sync.dma_start(
                out=lead_plane[32 * q : 32 * q + 4, :].bitcast(I32).rearrange("r (g n) -> r g n", g=4),
                in_=lead_scales.bitcast(I32)[:, 4 * q : 4 * q + 4, :].rearrange("g r n -> r g n"),
            )
        load_x(1, slice(0, S))
        nc.sync.dma_start(
            out=lead_codes[:].bitcast(I32).rearrange("p (g n) -> p g n", g=4),
            in_=lead_words.bitcast(I32).rearrange("g p n -> p g n"),
        )
        load_e(0)
        load_x(2, slice(0, S))
        for q in range(4):
            nc.sync.dma_start(
                out=inv_plane[32 * q : 32 * q + 4, :].bitcast(I32),
                in_=inv_scales.bitcast(I32)[0, 4 * q : 4 * q + 4, :],
            )
        nc.sync.dma_start(out=inv_codes[:].bitcast(I32), in_=inv_words.bitcast(I32)[0])
        for i in range(3, TILES):
            load_x(i, slice(0, S))
            if i % 2 == 1 and i < TILES - 1:
                load_e(i // 2)
        load_e(TILES // 2 - 1)

        w_col = kept([P, 16], F32, "w_col")
        w_wide = [kept([P, HALF], F32, "w_wide%d" % h) for h in range(2)]
        nc.scalar.activation(out=w_half[0:16, :], in_=w_rows[:], func=COPY, scale=0.5)

        def weight_columns():
            bank = next_bank()
            nc.tensor.transpose(bank[:, 0:P], w_half[:], ident[:])
            nc.vector.tensor_copy(out=w_col[:], in_=bank[:, 0:16])

        def weight_rows():
            for h in range(2):
                bank = next_bank()
                for j in range(4):
                    col = w_col[:, 8 * h + j : 8 * h + j + 1].to_broadcast([P, P])
                    nc.tensor.transpose(bank[:, P * j : P * (j + 1)], col, ident[:])
                nc.scalar.copy(out=w_wide[h][:], in_=bank[:])

        r_codes = [kept([P, 512], U32, "r_codes%d" % g) for g in range(GROUPS)]
        r_plane = [kept([P, 512], U8, "r_plane%d" % g) for g in range(GROUPS)]
        y_low = [kept([P, 4, HALF], F32, "y_low%d" % g) for g in range(GROUPS)]
        y_high = [[kept([P, 4, 256], F32, "y_high%d_%d" % (g, h)) for h in range(2)] for g in range(GROUPS)]
        y_bf = [[kept([P, HALF, 4], BF16, "y_bf%d_%d" % (g, h)) for h in range(2)] for g in range(GROUPS)]
        y_codes = [kept([P, NP], U32, "y_codes%d" % g) for g in range(GROUPS)]
        y_plane = [kept([P, NP], U8, "y_plane%d" % g) for g in range(GROUPS)]

        st = {}

        def put(key, val):
            st.setdefault(key, val)

        def sort_x(i):
            if i not in SORTED:
                return
            dealt = rotating([P, S // 2], F32, "x_dealt")
            nc.scalar.copy(
                out=dealt[:].rearrange("p (g u q) -> p g u q", g=4, u=2),
                in_=x[i][:].bitcast(F32).rearrange("p (g q u) -> p g u q", g=4, u=2),
            )
            put(("xs", i), dealt)

        def turn_x(i, h):
            words = x[i][:].bitcast(F32)
            bank = next_bank()
            for gl in range(2):
                g = 2 * h + gl
                for u in range(2):
                    slot = 2 * gl + u
                    if i in SORTED:
                        src = st[("xs", i)][:, 256 * g + P * u : 256 * g + P * (u + 1)]
                    else:
                        src = words[:, 256 * g + u : 256 * (g + 1) : 2]
                    nc.tensor.transpose(bank[:, P * slot : P * (slot + 1)], src, ident[:])
            put(("xt", i, h), bank)

        def copy_x(i, h):
            if h == 0:
                put(("xg", i), rotating([P, S], BF16, "x_grouped"))
            grouped = st[("xg", i)]
            nc.scalar.copy(
                out=grouped[:, 1024 * h : 1024 * (h + 1)].bitcast(F32).rearrange("p (g r u) -> p g r u", g=2, u=2),
                in_=st[("xt", i, h)][:].rearrange("p (g u r) -> p g r u", g=2, u=2),
            )

        def quantize_x(i):
            codes = rotating([P, 512], U32, "x_codes")
            plane = rotating([P, 512], U8, "x_plane")
            nc.vector.quantize_mx(out=codes[:].bitcast(FP8X4), scales=plane[:], in_=st[("xg", i)][:])
            put(("xq", i), (codes, plane))

        def predict(i):
            codes, plane = st[("xq", i)]
            bank = next_bank()
            for g in range(4):
                cols = slice(P * g, P * (g + 1))
                nc.tensor.matmul_mx(
                    out=bank[:],
                    lhsT=codes[:, cols].bitcast(FP8X4),
                    lhsT_scale=plane[:, cols],
                    rhs=lead_codes[:, 2 * C * g : 2 * C * (g + 1)].bitcast(FP4X4),
                    rhs_scale=lead_plane[:, C * g : C * (g + 1)],
                    start=(g == 0),
                    stop=(g == 3),
                )
            put(("pred", i), bank)

        def residual(i):
            r = rotating([P, C], BF16, "r")
            nc.vector.tensor_tensor(
                out=r[:].rearrange("p (u q e) -> p u q e", u=2, e=2),
                in0=e[i // 2][:, i % 2, :].rearrange("p (q u e) -> p u q e", u=2, e=2),
                in1=st[("pred", i)][:].rearrange("p (q u e) -> p u q e", u=2, e=2),
                op=ALU.subtract,
            )
            put(("r", i), r)

        def turn_r(i):
            words = st[("r", i)][:].bitcast(F32)
            bank = next_bank()
            for u in range(2):
                nc.tensor.transpose(bank[:, P * u : P * (u + 1)], words[:, P * u : P * (u + 1)], ident[:])
            put(("rt", i), bank)

        def copy_r(i):
            grouped = rotating([P, C], BF16, "r_grouped")
            nc.scalar.copy(
                out=grouped[:].bitcast(F32).rearrange("p (r u) -> p r u", u=2),
                in_=st[("rt", i)][:, 0 : 2 * P].rearrange("p (u r) -> p r u", u=2),
            )
            put(("rg", i), grouped)

        def quantize_r(i):
            g, cols = i // 4, slice(P * (i % 4), P * (i % 4 + 1))
            nc.vector.quantize_mx(
                out=r_codes[g][:, cols].bitcast(FP8X4), scales=r_plane[g][:, cols], in_=st[("rg", i)][:]
            )

        def low_matmul(i):
            g, cols = i // 4, slice(P * (i % 4), P * (i % 4 + 1))
            pair = []
            for h in range(2):
                bank = next_bank()
                n0 = NP * h
                nc.tensor.matmul_mx(
                    out=bank[:],
                    lhsT=r_codes[g][:, cols].bitcast(FP8X4),
                    lhsT_scale=r_plane[g][:, cols],
                    rhs=inv_codes[:, 2 * n0 : 2 * (n0 + HALF)].bitcast(FP4X4),
                    rhs_scale=inv_plane[:, n0 : n0 + HALF],
                    start=True,
                    stop=True,
                )
                pair.append(bank)
            put(("low", i), pair)

        def low_weigh(i):
            pair = []
            for h in range(2):
                z = rotating([P, HALF], F32, "z_low%d" % h)
                nc.vector.tensor_tensor(out=z[:], in0=st[("low", i)][h][:], in1=w_wide[h][:], op=ALU.mult)
                pair.append(z)
            put(("lowz", i), pair)

        def low_add(i):
            g, t = i // 4, i % 4
            a, b = st[("lowz", i)]
            nc.vector.tensor_tensor(out=y_low[g][:, t, :], in0=a[:], in1=b[:], op=ALU.add)
            nc.sync.dma_start(out=by_slot(out_0, g)[:, t, 0:HALF], in_=y_low[g][:, t, :])

        def cast_from_sbuf(on_vector, dst, src):
            out = dst.rearrange("p (c i) t -> p c t i", i=4)
            in_ = src.rearrange("p t (c i) -> p c t i", i=4)
            if on_vector:
                nc.vector.tensor_copy(out=out, in_=in_)
            else:
                nc.scalar.copy(out=out, in_=in_)

        def low_cast(g, j, on_vector=False):
            cols = slice(P * j, P * (j + 1))
            cast_from_sbuf(on_vector, y_bf[g][0][:, cols, :], y_low[g][:, :, cols])

        def high_matmul(n):
            g, j = n // 4, 4 + n % 4
            pair = []
            for h in range(2):
                bank = next_bank()
                n0 = NP * h + P * j
                nc.tensor.matmul_mx(
                    out=bank[:],
                    lhsT=inv_codes[:, 2 * n0 : 2 * (n0 + P)].bitcast(FP4X4),
                    lhsT_scale=inv_plane[:, n0 : n0 + P],
                    rhs=r_codes[g][:].bitcast(FP8X4),
                    rhs_scale=r_plane[g][:],
                    start=True,
                    stop=True,
                )
                pair.append(bank)
            put(("high", n), pair)

        def high_left(n):
            j = 4 + n % 4
            z = rotating([P, 512], F32, "z_high")
            nc.scalar.activation(out=z[:], in_=st[("high", n)][0][:], func=COPY, scale=w_col[:, j : j + 1])
            put(("highz", n), z)

        def high_sum(n):
            j = 12 + n % 4
            yt = rotating([P, 512], F32, "y_turned")
            nc.vector.scalar_tensor_tensor(
                out=yt[:],
                in0=st[("high", n)][1][:],
                scalar=w_col[:, j : j + 1],
                in1=st[("highz", n)][:],
                op0=ALU.mult,
                op1=ALU.add,
            )
            put(("yt", n), yt)

        def turn_y(n):
            bank = next_bank()
            for t in range(4):
                cols = slice(P * t, P * (t + 1))
                nc.tensor.transpose(bank[:, cols], st[("yt", n)][:, cols], ident[:])
            put(("y", n), bank)

        def copy_y(n, cast=True):
            g, j = n // 4, n % 4
            dst = y_high[g][j // 2]
            cols = slice(P * (j % 2), P * (j % 2 + 1))
            bank = st[("y", n)][:].rearrange("p (t m) -> p t m", t=4)
            nc.scalar.copy(out=dst[:, :, cols], in_=bank)
            if cast:
                nc.scalar.copy(out=y_bf[g][1][:, P * j : P * (j + 1), :], in_=bank.rearrange("p t m -> p m t"))
            if j % 2 == 1:
                c0 = HALF + 256 * (j // 2)
                nc.sync.dma_start(out=by_slot(out_0, g)[:, :, c0 : c0 + 256], in_=dst[:])

        def high_cast(n, on_vector=True):
            g, j = n // 4, n % 4
            src = y_high[g][j // 2][:, :, P * (j % 2) : P * (j % 2 + 1)]
            cast_from_sbuf(on_vector, y_bf[g][1][:, P * j : P * (j + 1), :], src)

        def quantize_y(g, h, c0=0, c1=HALF):
            cols = slice(HALF * h + c0, HALF * h + c1)
            nc.vector.quantize_mx(
                out=y_codes[g][:, cols].bitcast(FP8X4),
                scales=y_plane[g][:, cols],
                in_=y_bf[g][h][:, c0:c1, :].rearrange("p m t -> p (m t)"),
            )
            nc.sync.dma_start(
                out=out_1[g].rearrange("p m t -> p (m t)").bitcast(I32)[:, cols],
                in_=y_codes[g][:, cols].bitcast(I32),
            )

        def store_plane(g):
            for q in range(4):
                nc.sync.dma_start(
                    out=out_2.bitcast(I32)[g, 4 * q : 4 * q + 4, :],
                    in_=y_plane[g][32 * q : 32 * q + 4, :].bitcast(I32),
                )

        def live(i):
            return 0 <= i < TILES

        def when(fn, i, *more):
            if 0 <= i < TILES:
                fn(i, *more)

        def finish_low(g):
            quantize_y(g, 0)

        def finish_high(g):
            quantize_y(g, 1)
            store_plane(g)

        for s in range(TILES + 1):
            n = s - 5
            when(turn_x, s, 0)
            when(turn_r, s - 2)
            when(turn_x, s, 1)
            if s == 0:
                weight_columns()
            when(turn_y, n - 2)
            when(copy_x, s, 0)
            when(copy_r, s - 2)
            when(copy_x, s, 1)
            when(copy_y, n - 2)
            if s == 1:
                weight_rows()
            when(sort_x, s + 2)
            when(high_sum, n - 1)
            when(quantize_r, s - 2)
            when(low_add, s - 3)
            when(quantize_x, s)
            if s - 6 >= 0:
                low_cast((s - 6) // 4, (s - 6) % 4)
            when(predict, s - 1)
            when(low_matmul, s - 2)
            when(high_matmul, n)
            when(residual, s - 1)
            when(low_weigh, s - 2)
            when(high_left, n)
            if s == 9:
                finish_low(0)
            if s == 10:
                finish_high(0)
        turn_r(11)
        turn_y(6)
        copy_r(11)
        high_sum(7)
        turn_y(7)
        quantize_r(11)
        low_cast(1, 3)
        copy_y(6)
        copy_y(7)
        low_add(10)
        finish_low(1)
        low_matmul(11)
        high_matmul(8)
        high_matmul(9)
        low_weigh(11)
        high_left(8)
        high_left(9)
        high_matmul(10)
        high_left(10)
        finish_high(1)
        high_sum(8)
        low_add(11)
        high_sum(9)
        high_matmul(11)
        high_left(11)
        for j in range(1):
            low_cast(2, j)
        turn_y(8)
        turn_y(9)
        high_sum(10)
        high_sum(11)
        copy_y(8, False)
        copy_y(9, False)
        turn_y(10)
        turn_y(11)
        for j in range(1, 4):
            low_cast(2, j, True)
        copy_y(10, False)
        copy_y(11, True)
        finish_low(2)
        high_cast(8)
        high_cast(9)
        high_cast(10)
        quantize_y(2, 1, 0, 256)
        quantize_y(2, 1, 256, HALF)
        store_plane(2)
